import numpy as np
import ml_dtypes


def mxq(x, axis, fmt="e4m3"):
    dtype, down = {"e4m3": (ml_dtypes.float8_e4m3fn, 7), "e5m2": (ml_dtypes.float8_e5m2, 14)}[fmt]
    v = np.moveaxis(np.asarray(x, np.float32).astype(ml_dtypes.bfloat16).astype(np.float64), axis, -1)
    blocks = v.reshape(v.shape[:-1] + (-1, 32))
    amax = np.abs(blocks).max(-1, keepdims=True)
    byte = np.maximum(np.where(amax > 0, np.frexp(amax)[1] - 1 + 127, 0) - down, 1)
    scale = np.exp2(byte - 127.0)
    codes = (blocks / scale).astype(np.float32).astype(dtype).astype(np.float64)
    return np.moveaxis((codes * scale).reshape(v.shape), -1, axis)


WIDE = False


def mx_kscale(k):
    if not WIDE:
        return np.ones(k)
    levels = np.array([10, -10, 5, -5, 0])
    if k % 512:
        return np.exp2(np.random.permutation(np.resize(levels, k // 32))).repeat(32)
    a = np.empty((k // 512, 16))
    for p in range(k // 512):
        a[p, :8] = np.random.permutation(np.resize(levels, 8))
        for g in range(8):
            far = levels[np.abs(levels - a[p, g]) >= 10]
            a[p, g + 8] = far[np.random.randint(len(far))]
    return np.exp2(a.ravel()).repeat(32)


def f64(x):
    return np.asarray(x).astype(np.float64)


def striped(idx):
    return np.tile(idx.reshape(-1, 16).T, (8, 1)).astype(np.uint16)


def unstriped(offs):
    return offs[:16].T.reshape(-1).astype(np.int64)


def striped8(idx):
    return np.concatenate([x.reshape(-1, 16).T for x in idx]).astype(np.uint16)


def runs(offs, k):
    lists = np.stack([offs[16 * r : 16 * r + 16].T.reshape(-1) for r in range(8)]).astype(np.int64)
    return lists[np.arange(k) % 512 // 64]


def pack_weight(w):
    k, n = w.shape
    w = f64(np.asarray(w, np.float32).astype(ml_dtypes.bfloat16)).reshape(k // 32, 32, n)
    amax = np.abs(w).max(1)
    byte = np.clip(np.where(amax > 0, np.frexp(amax)[1] - 1 + 127 - 7, 1), 1, 254)
    scaled = (w * np.exp2(127.0 - byte)[:, None, :]).reshape(k, n).astype(np.float32)
    words = np.ascontiguousarray(scaled.reshape(k // 512, 128, 4, n).transpose(0, 1, 3, 2)).astype(ml_dtypes.float8_e4m3fn).view(np.uint8)
    return words, np.ascontiguousarray(byte.astype(np.uint8).reshape(k // 512, 16, n))


def unpack_weight(words, scales):
    g, p, n, _ = words.shape
    vals = np.ascontiguousarray(words).view(ml_dtypes.float8_e4m3fn).astype(np.float64) * np.repeat(np.exp2(scales.astype(np.float64) - 127.0), 8, axis=1)[..., None]
    return vals.transpose(0, 1, 3, 2).reshape(g * 512, n)


def sigmoid(v):
    return 1.0 / (1.0 + np.exp(-np.maximum(v, -700.0)))


K, T, S, N, G, H, U = 512, 2048, 256, 512, 2048, 512, 512


def setup_inputs():
    n = np.random.standard_normal
    s = mx_kscale(K)[:, None]
    u = mx_kscale(K)
    packed_xT = pack_weight(n((K, T)) * s)
    packed_dT = pack_weight(n((K, G)) / s)
    perm = np.random.permutation(U)
    return {
        "x_words": packed_xT[0],
        "x_scales": packed_xT[1],
        "d_words": packed_dT[0],
        "d_scales": packed_dT[1],
        "sl": np.random.uniform(1.0, 2.0, (H, 1)).astype(np.float32),
        "th": (0.5 * n((H, 1))).astype(np.float32),
        "gn": (np.random.uniform(0.5, 1.5, (H, 1)) * u[:, None]).astype(np.float32),
        "w1": (n((H, N)) / np.sqrt(H) / u[:, None]).astype(np.float32),
        "offs": striped8(np.random.randint(0, T, (8, S))),
        "ci": striped(np.random.permutation(G)[:H]),
        "n1": striped8(np.stack([np.random.permutation(S) for _ in range(8)])),
        "n2": striped(perm[:S]),
        "n3": striped(perm[S:]),
        "n4": striped(np.random.permutation(U)),
    }


def reference(x_words, x_scales, d_words, d_scales, sl, th, gn, w1, offs, ci, n1, n2, n3, n4):
    d_ci = unpack_weight(d_words, d_scales)[:, unstriped(ci)]
    xq = unpack_weight(x_words, x_scales)[np.arange(K)[:, None], runs(offs, K)]
    s = 0.0625 * (d_ci.T @ xq)
    sg = sigmoid(f64(sl) * (s[np.arange(H)[:, None], runs(n1, H)] - f64(th)))
    z = f64(gn) * (s * sg)
    h = mxq(f64(w1), 0, "e4m3").T @ mxq(z, 0, "e4m3")
    nw = 0.5 * h
    ph = np.zeros((N, U))
    ph[:, unstriped(n2)] = h
    pg = ph.copy()
    pg[:, unstriped(n3)] = nw
    return pg - pg[:, unstriped(n4)]

@@ -1,0 +1,212 @@
+from contextlib import ExitStack
+
+import concourse.mybir as mybir
+
+K, T, S, N, G, H, U = 512, 2048, 256, 512, 2048, 512, 512
+FLOPS = 2 * K * H * S + 2 * H * N * S
+
+F32 = mybir.dt.float32
+BF16 = mybir.dt.bfloat16
+I32 = mybir.dt.int32
+U32 = mybir.dt.uint32
+U16 = mybir.dt.uint16
+U8 = mybir.dt.uint8
+FP8X4 = mybir.dt.float8_e4m3fn_x4
+ACT = mybir.ActivationFunctionType
+ALU = mybir.AluOpType
+
+P = 128
+PACK = 4
+HALF = S // 2
+LIST_COL = 16
+PIECES = ((0, 64), (64, 64), (128, 128))
+
+
+def tile_picked_hwlesapagtwo_none_p_kernel(tc, x_words, x_scales, d_words, d_scales, sl, th, gn, w1, offs, ci, n1, n2, n3, n4, out):
+    nc = tc.nc
+    with ExitStack() as ctx:
+        keep = ctx.enter_context(tc.tile_pool(name="keep", bufs=1))
+        ring = ctx.enter_context(tc.tile_pool(name="ring", bufs=2))
+        psum_s = ctx.enter_context(tc.psum_pool(name="psum_s", bufs=1))
+        psum_h = ctx.enter_context(tc.psum_pool(name="psum_h", bufs=4))
+
+        def load_list(src, name):
+            tile = keep.tile(list(src.shape), U16, name=name)
+            nc.sync.dma_start(tile[:], src)
+            return tile
+
+        def entries(tile, start, count):
+            return tile[:, start // LIST_COL : (start + count) // LIST_COL]
+
+        xs_table = keep.tile([P, T], U8, name="xs_table", align_bytes=64)
+        ds_table = keep.tile([P, G], U8, name="ds_table", align_bytes=64)
+        xs_plane = keep.tile([P, S], U8, name="xs_plane", align_bytes=64)
+        nc.vector.memset(xs_table[:].bitcast(I32), 0)
+        nc.vector.memset(ds_table[:].bitcast(I32), 0)
+        nc.vector.memset(xs_plane[:].bitcast(I32), 0)
+
+        offs_t = load_list(offs, "offs_t")
+        nc.scalar.dma_start(xs_table[:].bitcast(I32)[0:P:8, :], x_scales[0].bitcast(I32))
+        ci_t = load_list(ci, "ci_t")
+        for q in range(4):
+            nc.scalar.dma_start(ds_table[:].bitcast(I32)[32 * q : 32 * q + 4, :], d_scales[0].bitcast(I32)[4 * q : 4 * q + 4, :])
+        dw_table = keep.tile([P, G], U32, name="dw_table", align_bytes=64)
+        nc.sync.dma_start(dw_table[:].bitcast(I32), d_words[0].rearrange("p n t -> p (n t)").bitcast(I32))
+        xw_table = keep.tile([P, T], U32, name="xw_table", align_bytes=64)
+        nc.sync.dma_start(xw_table[:].bitcast(I32), x_words[0].rearrange("p n t -> p (n t)").bitcast(I32))
+
+        w_rows = w1.rearrange("(p j) n -> p j n", j=PACK)
+        w_raw = []
+        for m in range(N // P):
+            raw = keep.tile([P, PACK, P], F32, name=f"w_raw{m}", tag=f"w_raw{m}")
+            nc.sync.dma_start(raw[:], w_rows[:, :, m * P : (m + 1) * P])
+            w_raw.append(raw)
+            if m == 0:
+                n1_t = load_list(n1, "n1_t")
+                n2_t = load_list(n2, "n2_t")
+            if m == 1:
+                n3_t = load_list(n3, "n3_t")
+        n4_t = load_list(n4, "n4_t")
+
+        sl_t = keep.tile([P, PACK], F32, name="sl_t")
+        th_t = keep.tile([P, PACK], F32, name="th_t")
+        gn_t = keep.tile([P, PACK], F32, name="gn_t")
+        for tile, src in ((sl_t, sl), (th_t, th), (gn_t, gn)):
+            nc.gpsimd.dma_start(tile[:], src.rearrange("(p t) o -> p (t o)", t=PACK))
+
+        pages = [keep.tile([P, U], F32, name=f"page{m}") for m in range(N // P)]
+        for page in pages:
+            nc.vector.memset(page[:], 0.0)
+
+        xs_picked = keep.tile([P, S], U8, name="xs_picked", align_bytes=64)
+        nc.vector.tensor_copy(xs_picked[:], xs_table[:].indirect(offs_t[:]))
+        for r in range(4):
+            nc.scalar.dma_start(xs_plane[:].bitcast(I32)[r:P:32, :], xs_picked[:].bitcast(I32)[8 * r : P : 32, :])
+
+        ds_picked = keep.tile([P, PACK, P], U8, name="ds_picked", align_bytes=64)
+        nc.vector.tensor_copy(ds_picked[:].rearrange("p t m -> p m t"), ds_table[:].indirect(ci_t[:]))
+        dw_picked = keep.tile([P, PACK, P], U32, name="dw_picked", align_bytes=64)
+        nc.vector.tensor_copy(dw_picked[:].rearrange("p t m -> p m t"), dw_table[:].indirect(ci_t[:]))
+        bias_t = keep.tile([P, PACK], F32, name="bias_t")
+        nc.vector.scalar_tensor_tensor(bias_t[:], sl_t[:], -1.0, th_t[:], ALU.mult, ALU.mult)
+        xw_picked = keep.tile([P, S], U32, name="xw_picked", align_bytes=64)
+        nc.vector.tensor_copy(xw_picked[:], xw_table[:].indirect(offs_t[:]))
+
+        scores = []
+        for t in range(PACK):
+            acc = psum_s.tile([P, S], F32, name=f"acc_s{t}")
+            nc.tensor.matmul_mx(
+                out=acc[:],
+                lhsT=dw_picked[:, t, :].bitcast(FP8X4),
+                lhsT_scale=ds_picked[:, t, :],
+                rhs=xw_picked[:].bitcast(FP8X4),
+                rhs_scale=xs_plane[:],
+                start=True,
+                stop=True,
+            )
+            score = keep.tile([P, S], F32, name=f"score{t}")
+            nc.vector.tensor_scalar(score[:], acc[:], 0.0625, None, ALU.mult)
+            scores.append(score)
+
+        def interleave(copy, dst, src):
+            copy(
+                out=dst[:].rearrange("p (c i) t -> p c t i", i=4),
+                in_=src[:].rearrange("p t (c i) -> p c t i", i=4),
+            )
+
+        wb0 = keep.tile([P, P, PACK], BF16, name="wb0", align_bytes=64)
+        interleave(nc.scalar.copy, wb0, w_raw[0])
+        gates = {}
+        for start, count in PIECES:
+            for t in range(PACK):
+                gate = keep.tile([P, count], F32, name=f"gate{start}_{t}", tag="w_raw0" if (start, t) == (0, 0) else f"gate{start}_{t}")
+                nc.scalar.activation(
+                    out=gate[:],
+                    in_=scores[t][:].indirect(entries(n1_t, start, count)),
+                    func=ACT.Sigmoid,
+                    scale=sl_t[:, t : t + 1],
+                    bias=bias_t[:, t : t + 1],
+                )
+                gates[start, t] = gate
+
+        z_codes = keep.tile([P, S], U32, name="z_codes", align_bytes=64)
+        z_scales = keep.tile([P, S], U8, name="z_scales", align_bytes=64)
+        w_codes = [keep.tile([P, P], U32, name=f"w_codes{m}", align_bytes=64) for m in range(N // P)]
+        w_scales = [keep.tile([P, P], U8, name=f"w_scales{m}", align_bytes=64) for m in range(N // P)]
+
+        def make_z(start, count):
+            cols = slice(start, start + count)
+            z = ring.tile([P, PACK, count], F32, name="z", bufs=1)
+            for t in range(PACK):
+                nc.vector.scalar_tensor_tensor(z[:, t, :], gates[start, t][:], gn_t[:, t : t + 1], scores[t][:, cols], ALU.mult, ALU.mult)
+            return z
+
+        def round_rows(copy, src, count, name):
+            grouped = ring.tile([P, count, PACK], BF16, name=name, align_bytes=64)
+            interleave(copy, grouped, src)
+            return grouped
+
+        def quantize(grouped, codes, scales):
+            nc.vector.quantize_mx(out=codes.bitcast(FP8X4), scales=scales, in_=grouped[:].rearrange("p c t -> p (c t)"))
+
+        hs = [keep.tile([P, S], F32, name=f"h{m}") for m in range(N // P)]
+        nws = [keep.tile([P, S], F32, name=f"nw{m}") for m in range(N // P)]
+
+        def product(m, start, count):
+            cols = slice(start, start + count)
+            acc = psum_h.tile([P, count], F32, name="acc_h")
+            nc.tensor.matmul_mx(
+                out=acc[:],
+                lhsT=w_codes[m][:].bitcast(FP8X4),
+                lhsT_scale=w_scales[m][:],
+                rhs=z_codes[:, cols].bitcast(FP8X4),
+                rhs_scale=z_scales[:, cols],
+                start=True,
+                stop=True,
+            )
+            nc.vector.tensor_copy(hs[m][:, cols], acc[:])
+            nc.vector.tensor_scalar(nws[m][:, cols], acc[:], 0.5, None, ALU.mult)
+
+        def put(m, values, slots, start, count):
+            nc.scalar.activation(out=pages[m][:].indirect(entries(slots, start, count)), in_=values[m][:, start : start + count], func=ACT.Copy)
+
+        def finish(m, start, count):
+            cols = slice(start, start + count)
+            fetched = ring.tile([P, count], F32, name="fetched", bufs=4)
+            nc.scalar.activation(out=fetched[:], in_=pages[m][:].indirect(entries(n4_t, start, count)), func=ACT.Copy)
+            result = ring.tile([P, count], F32, name="result", bufs=4)
+            nc.vector.tensor_tensor(result[:], pages[m][:, cols], fetched[:], ALU.subtract)
+            nc.sync.dma_start(out[m * P : (m + 1) * P, cols], result[:])
+
+        def quantize_z(start, count):
+            zb = round_rows(nc.vector.tensor_copy, make_z(start, count), count, "zb")
+            quantize(zb, z_codes[:, start : start + count], z_scales[:, start : start + count])
+
+        def quantize_w(m):
+            wb = round_rows(nc.vector.tensor_copy, w_raw[m], P, "wb")
+            quantize(wb, w_codes[m][:], w_scales[m][:])
+
+        quantize(wb0, w_codes[0][:], w_scales[0][:])
+        for piece, (start, count) in enumerate(PIECES):
+            quantize_z(start, count)
+            product(0, start, count)
+            if piece == 0:
+                quantize_w(1)
+            product(1, start, count)
+        for m in (2, 3):
+            quantize_w(m)
+            product(m, 0, S)
+
+        for start, count in PIECES:
+            for values, slots in ((hs, n2_t), (nws, n3_t)):
+                for m in (0, 1):
+                    put(m, values, slots, start, count)
+        for m in (2, 3):
+            put(m, hs, n2_t, 0, S)
+            finish(m - 2, 0, U // 2)
+            finish(m - 2, U // 2, U // 2)
+        for m in (2, 3):
+            put(m, nws, n3_t, 0, S)
+        for m in (2, 3):
+            finish(m, 0, U // 2)
+            finish(m, U // 2, U // 2)

@@ -40,32 +40,29 @@ def tile_picked_hwlesapagtwo_none_p_kernel(tc, x_words, x_scales, d_words, d_sca
 
         xs_table = keep.tile([P, T], U8, name="xs_table", align_bytes=64)
         ds_table = keep.tile([P, G], U8, name="ds_table", align_bytes=64)
-        xs_plane = keep.tile([P, S], U8, name="xs_plane", align_bytes=64)
         nc.vector.memset(xs_table[:].bitcast(I32), 0)
         nc.vector.memset(ds_table[:].bitcast(I32), 0)
-        nc.vector.memset(xs_plane[:].bitcast(I32), 0)
 
         offs_t = load_list(offs, "offs_t")
-        nc.scalar.dma_start(xs_table[:].bitcast(I32)[0:P:8, :], x_scales[0].bitcast(I32))
         ci_t = load_list(ci, "ci_t")
-        for q in range(4):
-            nc.scalar.dma_start(ds_table[:].bitcast(I32)[32 * q : 32 * q + 4, :], d_scales[0].bitcast(I32)[4 * q : 4 * q + 4, :])
+        nc.sync.dma_start(xs_table[:].bitcast(I32)[0:P:8, :], x_scales[0].bitcast(I32))
+        n1_t = load_list(n1, "n1_t")
+        nc.sync.dma_start(ds_table[:].bitcast(I32)[0:P:8, :], d_scales[0].bitcast(I32))
         dw_table = keep.tile([P, G], U32, name="dw_table", align_bytes=64)
         nc.sync.dma_start(dw_table[:].bitcast(I32), d_words[0].rearrange("p n t -> p (n t)").bitcast(I32))
-        xw_table = keep.tile([P, T], U32, name="xw_table", align_bytes=64)
+        xw_table = keep.tile([P, T], U32, name="xw_table", tag="xw_table", align_bytes=64)
         nc.sync.dma_start(xw_table[:].bitcast(I32), x_words[0].rearrange("p n t -> p (n t)").bitcast(I32))
 
         w_rows = w1.rearrange("(p j) n -> p j n", j=PACK)
-        w_raw = []
-        for m in range(N // P):
-            raw = keep.tile([P, PACK, P], F32, name=f"w_raw{m}", tag=f"w_raw{m}")
-            nc.sync.dma_start(raw[:], w_rows[:, :, m * P : (m + 1) * P])
-            w_raw.append(raw)
-            if m == 0:
-                n1_t = load_list(n1, "n1_t")
-                n2_t = load_list(n2, "n2_t")
-            if m == 1:
-                n3_t = load_list(n3, "n3_t")
+
+        def load_weights(first, blocks, tag):
+            raw = keep.tile([P, PACK, blocks * P], F32, name=f"w_raw{first}", tag=tag, align_bytes=64)
+            nc.sync.dma_start(raw[:], w_rows[:, :, first * P : (first + blocks) * P])
+            return [raw[:, :, b * P : (b + 1) * P] for b in range(blocks)]
+
+        w_raw = load_weights(0, 1, "w_raw0")
+        n2_t = load_list(n2, "n2_t")
+        n3_t = load_list(n3, "n3_t")
         n4_t = load_list(n4, "n4_t")
 
         sl_t = keep.tile([P, PACK], F32, name="sl_t")
@@ -78,48 +75,51 @@ def tile_picked_hwlesapagtwo_none_p_kernel(tc, x_words, x_scales, d_words, d_sca
         for page in pages:
             nc.vector.memset(page[:], 0.0)
 
-        xs_picked = keep.tile([P, S], U8, name="xs_picked", align_bytes=64)
-        nc.vector.tensor_copy(xs_picked[:], xs_table[:].indirect(offs_t[:]))
-        for r in range(4):
-            nc.scalar.dma_start(xs_plane[:].bitcast(I32)[r:P:32, :], xs_picked[:].bitcast(I32)[8 * r : P : 32, :])
+        scales_picked = keep.tile([P, S + H], U8, name="scales_picked", tag="scales_picked", align_bytes=64)
+        nc.vector.tensor_copy(scales_picked[:, 0:S], xs_table[:].indirect(offs_t[:]))
+        nc.vector.tensor_copy(scales_picked[:, S:].rearrange("p (t m) -> p m t", t=PACK), ds_table[:].indirect(ci_t[:]))
+        planes = keep.tile([P, S + H], U8, name="planes", align_bytes=64)
+        nc.vector.tensor_copy(planes[:].bitcast(I32), scales_picked[:].bitcast(I32))
+        for r in range(1, 4):
+            nc.scalar.dma_start(planes[:].bitcast(I32)[r:P:32, :], scales_picked[:].bitcast(I32)[8 * r : P : 32, :])
+        w_raw.extend(load_weights(1, 1, "scales_picked"))
 
-        ds_picked = keep.tile([P, PACK, P], U8, name="ds_picked", align_bytes=64)
-        nc.vector.tensor_copy(ds_picked[:].rearrange("p t m -> p m t"), ds_table[:].indirect(ci_t[:]))
-        dw_picked = keep.tile([P, PACK, P], U32, name="dw_picked", align_bytes=64)
+        dw_picked = keep.tile([P, PACK, P], U32, name="dw_picked", tag="dw_picked", align_bytes=64)
         nc.vector.tensor_copy(dw_picked[:].rearrange("p t m -> p m t"), dw_table[:].indirect(ci_t[:]))
-        bias_t = keep.tile([P, PACK], F32, name="bias_t")
-        nc.vector.scalar_tensor_tensor(bias_t[:], sl_t[:], -1.0, th_t[:], ALU.mult, ALU.mult)
         xw_picked = keep.tile([P, S], U32, name="xw_picked", align_bytes=64)
         nc.vector.tensor_copy(xw_picked[:], xw_table[:].indirect(offs_t[:]))
+        bias_t = keep.tile([P, PACK], F32, name="bias_t", tag="xw_table", align_bytes=64)
+        nc.vector.scalar_tensor_tensor(bias_t[:], sl_t[:], -1.0, th_t[:], ALU.mult, ALU.mult)
 
+        def interleave(copy, dst, src):
+            copy(
+                out=dst[:].rearrange("p (c i) t -> p c t i", i=4),
+                in_=src.rearrange("p t (c i) -> p c t i", i=4),
+            )
+
+        wb0 = keep.tile([P, P, PACK], BF16, name="wb0", align_bytes=64)
+        nc.gpsimd.tensor_copy(out=wb0[:], in_=w_raw[0].rearrange("p t c -> p c t"))
         scores = []
         for t in range(PACK):
             acc = psum_s.tile([P, S], F32, name=f"acc_s{t}")
             nc.tensor.matmul_mx(
                 out=acc[:],
                 lhsT=dw_picked[:, t, :].bitcast(FP8X4),
-                lhsT_scale=ds_picked[:, t, :],
+                lhsT_scale=planes[:, S + t * P : S + (t + 1) * P],
                 rhs=xw_picked[:].bitcast(FP8X4),
-                rhs_scale=xs_plane[:],
+                rhs_scale=planes[:, 0:S],
                 start=True,
                 stop=True,
             )
-            score = keep.tile([P, S], F32, name=f"score{t}")
+            score = keep.tile([P, S], F32, name=f"score{t}", align_bytes=64)
             nc.vector.tensor_scalar(score[:], acc[:], 0.0625, None, ALU.mult)
             scores.append(score)
 
-        def interleave(copy, dst, src):
-            copy(
-                out=dst[:].rearrange("p (c i) t -> p c t i", i=4),
-                in_=src[:].rearrange("p t (c i) -> p c t i", i=4),
-            )
-
-        wb0 = keep.tile([P, P, PACK], BF16, name="wb0", align_bytes=64)
-        interleave(nc.scalar.copy, wb0, w_raw[0])
+        w_raw.extend(load_weights(2, 2, "dw_picked"))
         gates = {}
         for start, count in PIECES:
             for t in range(PACK):
-                gate = keep.tile([P, count], F32, name=f"gate{start}_{t}", tag="w_raw0" if (start, t) == (0, 0) else f"gate{start}_{t}")
+                gate = keep.tile([P, count], F32, name=f"gate{start}_{t}", tag=f"gate{start}_{t}", align_bytes=64)
                 nc.scalar.activation(
                     out=gate[:],
                     in_=scores[t][:].indirect(entries(n1_t, start, count)),
@@ -131,7 +131,7 @@ def tile_picked_hwlesapagtwo_none_p_kernel(tc, x_words, x_scales, d_words, d_sca
 
         z_codes = keep.tile([P, S], U32, name="z_codes", align_bytes=64)
         z_scales = keep.tile([P, S], U8, name="z_scales", align_bytes=64)
-        w_codes = [keep.tile([P, P], U32, name=f"w_codes{m}", align_bytes=64) for m in range(N // P)]
+        w_codes = {}
         w_scales = [keep.tile([P, P], U8, name=f"w_scales{m}", align_bytes=64) for m in range(N // P)]
 
         def make_z(start, count):
@@ -139,10 +139,10 @@ def tile_picked_hwlesapagtwo_none_p_kernel(tc, x_words, x_scales, d_words, d_sca
             z = ring.tile([P, PACK, count], F32, name="z", bufs=1)
             for t in range(PACK):
                 nc.vector.scalar_tensor_tensor(z[:, t, :], gates[start, t][:], gn_t[:, t : t + 1], scores[t][:, cols], ALU.mult, ALU.mult)
-            return z
+            return z[:]
 
         def round_rows(copy, src, count, name):
-            grouped = ring.tile([P, count, PACK], BF16, name=name, align_bytes=64)
+            grouped = ring.tile([P, count, PACK], BF16, name=name, tag="grouped", bufs=1, align_bytes=64)
             interleave(copy, grouped, src)
             return grouped
 
@@ -178,23 +178,24 @@ def tile_picked_hwlesapagtwo_none_p_kernel(tc, x_words, x_scales, d_words, d_sca
             nc.vector.tensor_tensor(result[:], pages[m][:, cols], fetched[:], ALU.subtract)
             nc.sync.dma_start(out[m * P : (m + 1) * P, cols], result[:])
 
-        def quantize_z(start, count):
-            zb = round_rows(nc.vector.tensor_copy, make_z(start, count), count, "zb")
-            quantize(zb, z_codes[:, start : start + count], z_scales[:, start : start + count])
-
-        def quantize_w(m):
-            wb = round_rows(nc.vector.tensor_copy, w_raw[m], P, "wb")
+        def quantize_w(m, wb, tag):
+            w_codes[m] = keep.tile([P, P], U32, name=f"w_codes{m}", tag=tag, align_bytes=64)
             quantize(wb, w_codes[m][:], w_scales[m][:])
 
-        quantize(wb0, w_codes[0][:], w_scales[0][:])
+        def round_and_quantize_w(m):
+            quantize_w(m, round_rows(nc.vector.tensor_copy, w_raw[m], P, "wb"), f"w_codes{m}")
+
         for piece, (start, count) in enumerate(PIECES):
-            quantize_z(start, count)
+            zb = round_rows(nc.vector.tensor_copy, make_z(start, count), count, "zb")
+            if piece == 0:
+                quantize_w(0, wb0, "gate0_3")
+            quantize(zb, z_codes[:, start : start + count], z_scales[:, start : start + count])
             product(0, start, count)
             if piece == 0:
-                quantize_w(1)
+                round_and_quantize_w(1)
             product(1, start, count)
         for m in (2, 3):
-            quantize_w(m)
+            round_and_quantize_w(m)
             product(m, 0, S)
 
         for start, count in PIECES:
@@ -207,6 +208,8 @@ def tile_picked_hwlesapagtwo_none_p_kernel(tc, x_words, x_scales, d_words, d_sca
             finish(m - 2, U // 2, U // 2)
         for m in (2, 3):
             put(m, nws, n3_t, 0, S)
-        for m in (2, 3):
-            finish(m, 0, U // 2)
-            finish(m, U // 2, U // 2)
+        finish(2, 0, U // 2)
+        finish(2, U // 2, U // 2)
+        finish(3, 0, U // 2)
+        finish(3, U // 2, U // 4)
+        finish(3, 3 * U // 4, U // 4)

@@ -39,7 +39,7 @@ def tile_picked_hwlesapagtwo_none_p_kernel(tc, x_words, x_scales, d_words, d_sca
             return tile[:, start // LIST_COL : (start + count) // LIST_COL]
 
         xs_table = keep.tile([P, T], U8, name="xs_table", align_bytes=64)
-        ds_table = keep.tile([P, G], U8, name="ds_table", align_bytes=64)
+        ds_table = keep.tile([P, G], U8, name="ds_table", tag="ds_table", align_bytes=64)
         nc.vector.memset(xs_table[:].bitcast(I32), 0)
         nc.vector.memset(ds_table[:].bitcast(I32), 0)
 
@@ -47,6 +47,7 @@ def tile_picked_hwlesapagtwo_none_p_kernel(tc, x_words, x_scales, d_words, d_sca
         ci_t = load_list(ci, "ci_t")
         nc.sync.dma_start(xs_table[:].bitcast(I32)[0:P:8, :], x_scales[0].bitcast(I32))
         n1_t = load_list(n1, "n1_t")
+        n2_t = load_list(n2, "n2_t")
         nc.sync.dma_start(ds_table[:].bitcast(I32)[0:P:8, :], d_scales[0].bitcast(I32))
         dw_table = keep.tile([P, G], U32, name="dw_table", align_bytes=64)
         nc.sync.dma_start(dw_table[:].bitcast(I32), d_words[0].rearrange("p n t -> p (n t)").bitcast(I32))
@@ -60,8 +61,6 @@ def tile_picked_hwlesapagtwo_none_p_kernel(tc, x_words, x_scales, d_words, d_sca
             nc.sync.dma_start(raw[:], w_rows[:, :, first * P : (first + blocks) * P])
             return [raw[:, :, b * P : (b + 1) * P] for b in range(blocks)]
 
-        w_raw = load_weights(0, 1, "w_raw0")
-        n2_t = load_list(n2, "n2_t")
         n3_t = load_list(n3, "n3_t")
         n4_t = load_list(n4, "n4_t")
 
@@ -71,25 +70,28 @@ def tile_picked_hwlesapagtwo_none_p_kernel(tc, x_words, x_scales, d_words, d_sca
         for tile, src in ((sl_t, sl), (th_t, th), (gn_t, gn)):
             nc.gpsimd.dma_start(tile[:], src.rearrange("(p t) o -> p (t o)", t=PACK))
 
+        planes = keep.tile([P, S + H], U8, name="planes", align_bytes=64)
+        nc.vector.memset(planes[:].bitcast(I32), 0)
         pages = [keep.tile([P, U], F32, name=f"page{m}") for m in range(N // P)]
         for page in pages:
             nc.vector.memset(page[:], 0.0)
 
-        scales_picked = keep.tile([P, S + H], U8, name="scales_picked", tag="scales_picked", align_bytes=64)
+        scales_picked = keep.tile([P, S + H], U8, name="scales_picked", align_bytes=64)
         nc.vector.tensor_copy(scales_picked[:, 0:S], xs_table[:].indirect(offs_t[:]))
         nc.vector.tensor_copy(scales_picked[:, S:].rearrange("p (t m) -> p m t", t=PACK), ds_table[:].indirect(ci_t[:]))
-        planes = keep.tile([P, S + H], U8, name="planes", align_bytes=64)
-        nc.vector.tensor_copy(planes[:].bitcast(I32), scales_picked[:].bitcast(I32))
-        for r in range(1, 4):
-            nc.scalar.dma_start(planes[:].bitcast(I32)[r:P:32, :], scales_picked[:].bitcast(I32)[8 * r : P : 32, :])
-        w_raw.extend(load_weights(1, 1, "scales_picked"))
+        for r in range(4):
+            nc.sync.dma_start(planes[:].bitcast(I32)[r:P:32, :], scales_picked[:].bitcast(I32)[8 * r : P : 32, :])
+        w_raw = load_weights(0, 2, "ds_table")
 
         dw_picked = keep.tile([P, PACK, P], U32, name="dw_picked", tag="dw_picked", align_bytes=64)
         nc.vector.tensor_copy(dw_picked[:].rearrange("p t m -> p m t"), dw_table[:].indirect(ci_t[:]))
         xw_picked = keep.tile([P, S], U32, name="xw_picked", align_bytes=64)
         nc.vector.tensor_copy(xw_picked[:], xw_table[:].indirect(offs_t[:]))
-        bias_t = keep.tile([P, PACK], F32, name="bias_t", tag="xw_table", align_bytes=64)
-        nc.vector.scalar_tensor_tensor(bias_t[:], sl_t[:], -1.0, th_t[:], ALU.mult, ALU.mult)
+        row_t = keep.tile([P, 2 * PACK], F32, name="row_t", tag="xw_table", align_bytes=64)
+        bias_t = row_t[:, 0:PACK]
+        gain_t = row_t[:, PACK:]
+        nc.vector.scalar_tensor_tensor(bias_t, sl_t[:], -1.0, th_t[:], ALU.mult, ALU.mult)
+        nc.vector.tensor_scalar(gain_t, gn_t[:], 0.0625, None, ALU.mult)
 
         def interleave(copy, dst, src):
             copy(
@@ -97,9 +99,13 @@ def tile_picked_hwlesapagtwo_none_p_kernel(tc, x_words, x_scales, d_words, d_sca
                 in_=src.rearrange("p t (c i) -> p c t i", i=4),
             )
 
-        wb0 = keep.tile([P, P, PACK], BF16, name="wb0", align_bytes=64)
-        nc.gpsimd.tensor_copy(out=wb0[:], in_=w_raw[0].rearrange("p t c -> p c t"))
+        wb = []
+        for m in range(2):
+            early = keep.tile([P, P, PACK], BF16, name=f"wb{m}", align_bytes=64)
+            nc.gpsimd.tensor_copy(out=early[:], in_=w_raw[m].rearrange("p t c -> p c t"))
+            wb.append(early)
         scores = []
+        sums = []
         for t in range(PACK):
             acc = psum_s.tile([P, S], F32, name=f"acc_s{t}")
             nc.tensor.matmul_mx(
@@ -114,6 +120,7 @@ def tile_picked_hwlesapagtwo_none_p_kernel(tc, x_words, x_scales, d_words, d_sca
             score = keep.tile([P, S], F32, name=f"score{t}", align_bytes=64)
             nc.vector.tensor_scalar(score[:], acc[:], 0.0625, None, ALU.mult)
             scores.append(score)
+            sums.append(acc)
 
         w_raw.extend(load_weights(2, 2, "dw_picked"))
         gates = {}
@@ -138,11 +145,11 @@ def tile_picked_hwlesapagtwo_none_p_kernel(tc, x_words, x_scales, d_words, d_sca
             cols = slice(start, start + count)
             z = ring.tile([P, PACK, count], F32, name="z", bufs=1)
             for t in range(PACK):
-                nc.vector.scalar_tensor_tensor(z[:, t, :], gates[start, t][:], gn_t[:, t : t + 1], scores[t][:, cols], ALU.mult, ALU.mult)
+                nc.vector.scalar_tensor_tensor(z[:, t, :], gates[start, t][:], gain_t[:, t : t + 1], sums[t][:, cols], ALU.mult, ALU.mult)
             return z[:]
 
-        def round_rows(copy, src, count, name):
-            grouped = ring.tile([P, count, PACK], BF16, name=name, tag="grouped", bufs=1, align_bytes=64)
+        def round_rows(copy, src, count, name, tag="grouped"):
+            grouped = keep.tile([P, count, PACK], BF16, name=name, tag=tag, align_bytes=64)
             interleave(copy, grouped, src)
             return grouped
 
@@ -150,7 +157,6 @@ def tile_picked_hwlesapagtwo_none_p_kernel(tc, x_words, x_scales, d_words, d_sca
             nc.vector.quantize_mx(out=codes.bitcast(FP8X4), scales=scales, in_=grouped[:].rearrange("p c t -> p (c t)"))
 
         hs = [keep.tile([P, S], F32, name=f"h{m}") for m in range(N // P)]
-        nws = [keep.tile([P, S], F32, name=f"nw{m}") for m in range(N // P)]
 
         def product(m, start, count):
             cols = slice(start, start + count)
@@ -165,16 +171,15 @@ def tile_picked_hwlesapagtwo_none_p_kernel(tc, x_words, x_scales, d_words, d_sca
                 stop=True,
             )
             nc.vector.tensor_copy(hs[m][:, cols], acc[:])
-            nc.vector.tensor_scalar(nws[m][:, cols], acc[:], 0.5, None, ALU.mult)
 
-        def put(m, values, slots, start, count):
-            nc.scalar.activation(out=pages[m][:].indirect(entries(slots, start, count)), in_=values[m][:, start : start + count], func=ACT.Copy)
+        def put(m, factor, slots, start, count):
+            nc.scalar.activation(out=pages[m][:].indirect(entries(slots, start, count)), in_=hs[m][:, start : start + count], func=ACT.Copy, scale=factor)
 
         def finish(m, start, count):
             cols = slice(start, start + count)
-            fetched = ring.tile([P, count], F32, name="fetched", bufs=4)
+            fetched = ring.tile([P, count], F32, name="fetched", bufs=9)
             nc.scalar.activation(out=fetched[:], in_=pages[m][:].indirect(entries(n4_t, start, count)), func=ACT.Copy)
-            result = ring.tile([P, count], F32, name="result", bufs=4)
+            result = ring.tile([P, count], F32, name="result", bufs=9)
             nc.vector.tensor_tensor(result[:], pages[m][:, cols], fetched[:], ALU.subtract)
             nc.sync.dma_start(out[m * P : (m + 1) * P, cols], result[:])
 
@@ -186,28 +191,28 @@ def tile_picked_hwlesapagtwo_none_p_kernel(tc, x_words, x_scales, d_words, d_sca
             quantize_w(m, round_rows(nc.vector.tensor_copy, w_raw[m], P, "wb"), f"w_codes{m}")
 
         for piece, (start, count) in enumerate(PIECES):
-            zb = round_rows(nc.vector.tensor_copy, make_z(start, count), count, "zb")
+            zb = round_rows(nc.vector.tensor_copy, make_z(start, count), count, "zb", "zb0" if piece == 0 else "grouped")
             if piece == 0:
-                quantize_w(0, wb0, "gate0_3")
+                quantize_w(0, wb[0], "gate0_3")
             quantize(zb, z_codes[:, start : start + count], z_scales[:, start : start + count])
-            product(0, start, count)
             if piece == 0:
-                round_and_quantize_w(1)
+                quantize_w(1, wb[1], "zb0")
+            product(0, start, count)
             product(1, start, count)
         for m in (2, 3):
             round_and_quantize_w(m)
             product(m, 0, S)
 
         for start, count in PIECES:
-            for values, slots in ((hs, n2_t), (nws, n3_t)):
+            for factor, slots in ((1.0, n2_t), (0.5, n3_t)):
                 for m in (0, 1):
-                    put(m, values, slots, start, count)
+                    put(m, factor, slots, start, count)
         for m in (2, 3):
-            put(m, hs, n2_t, 0, S)
+            put(m, 1.0, n2_t, 0, S)
             finish(m - 2, 0, U // 2)
             finish(m - 2, U // 2, U // 2)
         for m in (2, 3):
-            put(m, nws, n3_t, 0, S)
+            put(m, 0.5, n3_t, 0, S)
         finish(2, 0, U // 2)
         finish(2, U // 2, U // 2)
         finish(3, 0, U // 2)

from contextlib import ExitStack

import concourse.mybir as mybir

K, T, S, N, G, H, U = 512, 2048, 256, 512, 2048, 512, 512
FLOPS = 2 * K * H * S + 2 * H * N * S

F32 = mybir.dt.float32
BF16 = mybir.dt.bfloat16
I32 = mybir.dt.int32
U32 = mybir.dt.uint32
U16 = mybir.dt.uint16
U8 = mybir.dt.uint8
FP8X4 = mybir.dt.float8_e4m3fn_x4
ACT = mybir.ActivationFunctionType
ALU = mybir.AluOpType

P = 128
PACK = 4
HALF = S // 2
LIST_COL = 16
PIECES = ((0, 64), (64, 64), (128, 128))


def tile_picked_hwlesapagtwo_none_p_kernel(tc, x_words, x_scales, d_words, d_scales, sl, th, gn, w1, offs, ci, n1, n2, n3, n4, out):
    nc = tc.nc
    with ExitStack() as ctx:
        keep = ctx.enter_context(tc.tile_pool(name="keep", bufs=1))
        ring = ctx.enter_context(tc.tile_pool(name="ring", bufs=2))
        psum_s = ctx.enter_context(tc.psum_pool(name="psum_s", bufs=1))
        psum_h = ctx.enter_context(tc.psum_pool(name="psum_h", bufs=4))

        def load_list(src, name):
            tile = keep.tile(list(src.shape), U16, name=name)
            nc.sync.dma_start(tile[:], src)
            return tile

        def entries(tile, start, count):
            return tile[:, start // LIST_COL : (start + count) // LIST_COL]

        xs_table = keep.tile([P, T], U8, name="xs_table", align_bytes=64)
        ds_table = keep.tile([P, G], U8, name="ds_table", tag="ds_table", align_bytes=64)
        nc.vector.memset(xs_table[:].bitcast(I32), 0)
        nc.vector.memset(ds_table[:].bitcast(I32), 0)

        offs_t = load_list(offs, "offs_t")
        ci_t = load_list(ci, "ci_t")
        nc.sync.dma_start(xs_table[:].bitcast(I32)[0:P:8, :], x_scales[0].bitcast(I32))
        n1_t = load_list(n1, "n1_t")
        n2_t = load_list(n2, "n2_t")
        nc.sync.dma_start(ds_table[:].bitcast(I32)[0:P:8, :], d_scales[0].bitcast(I32))
        dw_table = keep.tile([P, G], U32, name="dw_table", align_bytes=64)
        nc.sync.dma_start(dw_table[:].bitcast(I32), d_words[0].rearrange("p n t -> p (n t)").bitcast(I32))
        xw_table = keep.tile([P, T], U32, name="xw_table", tag="xw_table", align_bytes=64)
        nc.sync.dma_start(xw_table[:].bitcast(I32), x_words[0].rearrange("p n t -> p (n t)").bitcast(I32))

        w_rows = w1.rearrange("(p j) n -> p j n", j=PACK)

        def load_weights(first, blocks, tag):
            raw = keep.tile([P, PACK, blocks * P], F32, name=f"w_raw{first}", tag=tag, align_bytes=64)
            nc.sync.dma_start(raw[:], w_rows[:, :, first * P : (first + blocks) * P])
            return [raw[:, :, b * P : (b + 1) * P] for b in range(blocks)]

        n3_t = load_list(n3, "n3_t")
        n4_t = load_list(n4, "n4_t")

        sl_t = keep.tile([P, PACK], F32, name="sl_t")
        th_t = keep.tile([P, PACK], F32, name="th_t")
        gn_t = keep.tile([P, PACK], F32, name="gn_t")
        for tile, src in ((sl_t, sl), (th_t, th), (gn_t, gn)):
            nc.gpsimd.dma_start(tile[:], src.rearrange("(p t) o -> p (t o)", t=PACK))

        planes = keep.tile([P, S + H], U8, name="planes", align_bytes=64)
        nc.vector.memset(planes[:].bitcast(I32), 0)
        pages = [keep.tile([P, U], F32, name=f"page{m}") for m in range(N // P)]
        for page in pages:
            nc.vector.memset(page[:], 0.0)

        scales_picked = keep.tile([P, S + H], U8, name="scales_picked", align_bytes=64)
        nc.vector.tensor_copy(scales_picked[:, 0:S], xs_table[:].indirect(offs_t[:]))
        nc.vector.tensor_copy(scales_picked[:, S:].rearrange("p (t m) -> p m t", t=PACK), ds_table[:].indirect(ci_t[:]))
        for r in range(4):
            nc.sync.dma_start(planes[:].bitcast(I32)[r:P:32, :], scales_picked[:].bitcast(I32)[8 * r : P : 32, :])
        w_raw = load_weights(0, 2, "ds_table")

        dw_picked = keep.tile([P, PACK, P], U32, name="dw_picked", tag="dw_picked", align_bytes=64)
        nc.vector.tensor_copy(dw_picked[:].rearrange("p t m -> p m t"), dw_table[:].indirect(ci_t[:]))
        xw_picked = keep.tile([P, S], U32, name="xw_picked", align_bytes=64)
        nc.vector.tensor_copy(xw_picked[:], xw_table[:].indirect(offs_t[:]))
        row_t = keep.tile([P, 2 * PACK], F32, name="row_t", tag="xw_table", align_bytes=64)
        bias_t = row_t[:, 0:PACK]
        gain_t = row_t[:, PACK:]
        nc.vector.scalar_tensor_tensor(bias_t, sl_t[:], -1.0, th_t[:], ALU.mult, ALU.mult)
        nc.vector.tensor_scalar(gain_t, gn_t[:], 0.0625, None, ALU.mult)

        def interleave(copy, dst, src):
            copy(
                out=dst[:].rearrange("p (c i) t -> p c t i", i=4),
                in_=src.rearrange("p t (c i) -> p c t i", i=4),
            )

        wb = []
        for m in range(2):
            early = keep.tile([P, P, PACK], BF16, name=f"wb{m}", align_bytes=64)
            nc.gpsimd.tensor_copy(out=early[:], in_=w_raw[m].rearrange("p t c -> p c t"))
            wb.append(early)
        scores = []
        sums = []
        for t in range(PACK):
            acc = psum_s.tile([P, S], F32, name=f"acc_s{t}")
            nc.tensor.matmul_mx(
                out=acc[:],
                lhsT=dw_picked[:, t, :].bitcast(FP8X4),
                lhsT_scale=planes[:, S + t * P : S + (t + 1) * P],
                rhs=xw_picked[:].bitcast(FP8X4),
                rhs_scale=planes[:, 0:S],
                start=True,
                stop=True,
            )
            score = keep.tile([P, S], F32, name=f"score{t}", align_bytes=64)
            nc.vector.tensor_scalar(score[:], acc[:], 0.0625, None, ALU.mult)
            scores.append(score)
            sums.append(acc)

        w_raw.extend(load_weights(2, 2, "dw_picked"))
        gates = {}
        for start, count in PIECES:
            for t in range(PACK):
                gate = keep.tile([P, count], F32, name=f"gate{start}_{t}", tag=f"gate{start}_{t}", align_bytes=64)
                nc.scalar.activation(
                    out=gate[:],
                    in_=scores[t][:].indirect(entries(n1_t, start, count)),
                    func=ACT.Sigmoid,
                    scale=sl_t[:, t : t + 1],
                    bias=bias_t[:, t : t + 1],
                )
                gates[start, t] = gate

        z_codes = keep.tile([P, S], U32, name="z_codes", align_bytes=64)
        z_scales = keep.tile([P, S], U8, name="z_scales", align_bytes=64)
        w_codes = {}
        w_scales = [keep.tile([P, P], U8, name=f"w_scales{m}", align_bytes=64) for m in range(N // P)]

        def make_z(start, count):
            cols = slice(start, start + count)
            z = ring.tile([P, PACK, count], F32, name="z", bufs=1)
            for t in range(PACK):
                nc.vector.scalar_tensor_tensor(z[:, t, :], gates[start, t][:], gain_t[:, t : t + 1], sums[t][:, cols], ALU.mult, ALU.mult)
            return z[:]

        def round_rows(copy, src, count, name, tag="grouped"):
            grouped = keep.tile([P, count, PACK], BF16, name=name, tag=tag, align_bytes=64)
            interleave(copy, grouped, src)
            return grouped

        def quantize(grouped, codes, scales):
            nc.vector.quantize_mx(out=codes.bitcast(FP8X4), scales=scales, in_=grouped[:].rearrange("p c t -> p (c t)"))

        hs = [keep.tile([P, S], F32, name=f"h{m}") for m in range(N // P)]

        def product(m, start, count):
            cols = slice(start, start + count)
            acc = psum_h.tile([P, count], F32, name="acc_h")
            nc.tensor.matmul_mx(
                out=acc[:],
                lhsT=w_codes[m][:].bitcast(FP8X4),
                lhsT_scale=w_scales[m][:],
                rhs=z_codes[:, cols].bitcast(FP8X4),
                rhs_scale=z_scales[:, cols],
                start=True,
                stop=True,
            )
            nc.vector.tensor_copy(hs[m][:, cols], acc[:])

        def put(m, factor, slots, start, count):
            nc.scalar.activation(out=pages[m][:].indirect(entries(slots, start, count)), in_=hs[m][:, start : start + count], func=ACT.Copy, scale=factor)

        def finish(m, start, count):
            cols = slice(start, start + count)
            fetched = ring.tile([P, count], F32, name="fetched", bufs=9)
            nc.scalar.activation(out=fetched[:], in_=pages[m][:].indirect(entries(n4_t, start, count)), func=ACT.Copy)
            result = ring.tile([P, count], F32, name="result", bufs=9)
            nc.vector.tensor_tensor(result[:], pages[m][:, cols], fetched[:], ALU.subtract)
            nc.sync.dma_start(out[m * P : (m + 1) * P, cols], result[:])

        def quantize_w(m, wb, tag):
            w_codes[m] = keep.tile([P, P], U32, name=f"w_codes{m}", tag=tag, align_bytes=64)
            quantize(wb, w_codes[m][:], w_scales[m][:])

        def round_and_quantize_w(m):
            quantize_w(m, round_rows(nc.vector.tensor_copy, w_raw[m], P, "wb"), f"w_codes{m}")

        for piece, (start, count) in enumerate(PIECES):
            zb = round_rows(nc.vector.tensor_copy, make_z(start, count), count, "zb", "zb0" if piece == 0 else "grouped")
            if piece == 0:
                quantize_w(0, wb[0], "gate0_3")
            quantize(zb, z_codes[:, start : start + count], z_scales[:, start : start + count])
            if piece == 0:
                quantize_w(1, wb[1], "zb0")
            product(0, start, count)
            product(1, start, count)
        for m in (2, 3):
            round_and_quantize_w(m)
            product(m, 0, S)

        for start, count in PIECES:
            for factor, slots in ((1.0, n2_t), (0.5, n3_t)):
                for m in (0, 1):
                    put(m, factor, slots, start, count)
        for m in (2, 3):
            put(m, 1.0, n2_t, 0, S)
            finish(m - 2, 0, U // 2)
            finish(m - 2, U // 2, U // 2)
        for m in (2, 3):
            put(m, 0.5, n3_t, 0, S)
        finish(2, 0, U // 2)
        finish(2, U // 2, U // 2)
        finish(3, 0, U // 2)
        finish(3, U // 2, U // 4)
        finish(3, 3 * U // 4, U // 4)
